import numpy as np
import ml_dtypes


def mxq(x, axis, fmt="e4m3"):
    dtype, down = {"e4m3": (ml_dtypes.float8_e4m3fn, 7), "e5m2": (ml_dtypes.float8_e5m2, 14)}[fmt]
    v = np.moveaxis(np.asarray(x, np.float32).astype(ml_dtypes.bfloat16).astype(np.float64), axis, -1)
    blocks = v.reshape(v.shape[:-1] + (-1, 32))
    amax = np.abs(blocks).max(-1, keepdims=True)
    byte = np.maximum(np.where(amax > 0, np.frexp(amax)[1] - 1 + 127, 0) - down, 1)
    scale = np.exp2(byte - 127.0)
    codes = (blocks / scale).astype(np.float32).astype(dtype).astype(np.float64)
    return np.moveaxis((codes * scale).reshape(v.shape), -1, axis)


WIDE = False


def mx_kscale(k):
    if not WIDE:
        return np.ones(k)
    levels = np.array([10, -10, 5, -5, 0])
    if k % 512:
        return np.exp2(np.random.permutation(np.resize(levels, k // 32))).repeat(32)
    a = np.empty((k // 512, 16))
    for p in range(k // 512):
        a[p, :8] = np.random.permutation(np.resize(levels, 8))
        for g in range(8):
            far = levels[np.abs(levels - a[p, g]) >= 10]
            a[p, g + 8] = far[np.random.randint(len(far))]
    return np.exp2(a.ravel()).repeat(32)


def f64(x):
    return np.asarray(x).astype(np.float64)


def striped(idx):
    return np.tile(idx.reshape(-1, 16).T, (8, 1)).astype(np.uint16)


def unstriped(offs):
    return offs[:16].T.reshape(-1).astype(np.int64)


def pack_weight(w):
    k, n = w.shape
    w = f64(np.asarray(w, np.float32).astype(ml_dtypes.bfloat16)).reshape(k // 32, 32, n)
    amax = np.abs(w).max(1)
    byte = np.clip(np.where(amax > 0, np.frexp(amax)[1] - 1 + 127 - 7, 1), 1, 254)
    scaled = (w * np.exp2(127.0 - byte)[:, None, :]).reshape(k, n).astype(np.float32)
    words = np.ascontiguousarray(scaled.reshape(k // 512, 128, 4, n).transpose(0, 1, 3, 2)).astype(ml_dtypes.float8_e4m3fn).view(np.uint8)
    return words, np.ascontiguousarray(byte.astype(np.uint8).reshape(k // 512, 16, n))


def unpack_weight(words, scales):
    g, p, n, _ = words.shape
    vals = np.ascontiguousarray(words).view(ml_dtypes.float8_e4m3fn).astype(np.float64) * np.repeat(np.exp2(scales.astype(np.float64) - 127.0), 8, axis=1)[..., None]
    return vals.transpose(0, 1, 3, 2).reshape(g * 512, n)


def relu(v):
    return np.maximum(v, 0.0)


K, T, S, V, D, W = 1024, 2048, 512, 128, 4, 512


def setup_inputs():
    n = np.random.standard_normal
    s = mx_kscale(K)[:, None]
    packed_xT = pack_weight(n((K, T)) * s)
    return {
        "x_words": packed_xT[0],
        "x_scales": packed_xT[1],
        "lc": (n((K, W)) / np.sqrt(K) / s).astype(np.float32),
        "th": (n((K, V)) / np.sqrt(K) / s).astype(np.float32),
        "alpha": (np.random.uniform(0.3, 1.5, (S, 1))).astype(np.float32),
        "offs": striped(np.random.permutation(T)[:S]),
    }


def reference(x_words, x_scales, lc, th, alpha, offs):
    xq = unpack_weight(x_words, x_scales)[:, unstriped(offs)]
    thq = mxq(f64(th), 0, "e4m3")
    y = xq.T @ thq
    lcq = mxq(f64(lc), 0, "e4m3")
    z = xq.T @ lcq
    z2 = (z) ** 2
    bon = np.sqrt(z2.reshape(len(z2), -1, D).sum(axis=2) + 0.05)
    ucb = y + f64(alpha) * bon
    best = y.max(axis=1, keepdims=True)
    return relu(ucb - best)

@@ -1,0 +1,221 @@
+from contextlib import ExitStack
+
+import concourse.mybir as mybir
+from concourse.masks import make_identity
+
+K, T, S, V, D, W = 1024, 2048, 512, 128, 4, 512
+FLOPS = 2 * K * S * (V + W)
+
+F32 = mybir.dt.float32
+BF16 = mybir.dt.bfloat16
+I32 = mybir.dt.int32
+U32 = mybir.dt.uint32
+U16 = mybir.dt.uint16
+U8 = mybir.dt.uint8
+FP8X4 = mybir.dt.float8_e4m3fn_x4
+ACT = mybir.ActivationFunctionType
+ALU = mybir.AluOpType
+AX = mybir.AxisListType
+
+P = 128
+PACK = 4
+K_PASS = P * PACK
+PASSES = K // K_PASS
+TILES = S // P
+CW = 128
+CHUNKS = W // CW
+ARMS = CW // D
+LAST = CHUNKS - 1
+EARLY = 1
+
+
+def tile_picked_ylucb_gain_p_kernel(tc, x_words, x_scales, lc, th, alpha, offs, out):
+    nc = tc.nc
+    with ExitStack() as ctx:
+        keep = ctx.enter_context(tc.tile_pool(name="keep", bufs=1))
+        psum = ctx.enter_context(tc.psum_pool(name="psum", bufs=1))
+
+        def sbuf(shape, dtype, name, slot=None):
+            return keep.tile(shape, dtype, name=name, tag=slot or name, align_bytes=64)
+
+        scale_table = sbuf([P, T], U8, "scale_table")
+        nc.gpsimd.memset(scale_table[:].bitcast(I32), 0)
+
+        def load_scale_rows(queue, q):
+            queue.dma_start(
+                scale_table[32 * q : 32 * q + 4 * PASSES, :].bitcast(I32),
+                x_scales[:, 4 * q : 4 * q + 4, :].bitcast(I32),
+            )
+
+
+        lc_raw = {}
+
+        def load_chunk(c):
+            for g in range(PASSES):
+                raw = sbuf([P, PACK, CW], F32, f"lc_raw{c}_{g}")
+                rows = lc[g * K_PASS : (g + 1) * K_PASS, c * CW : (c + 1) * CW]
+                nc.sync.dma_start(raw[:], rows.rearrange("(p j) c -> p j c", j=PACK))
+                lc_raw[c, g] = raw
+
+        offsets = keep.tile([P, S // 16], U16, name="offsets")
+        nc.sync.dma_start(offsets[:], offs)
+        th_raw = sbuf([P, PASSES, PACK * V], F32, "th_raw")
+        nc.sync.dma_start(th_raw[:], th.rearrange("(g p j) v -> p g (j v)", g=PASSES, j=PACK))
+        load_scale_rows(nc.sync, 0)
+        load_scale_rows(nc.sync, 1)
+        load_scale_rows(nc.sync, 2)
+        load_scale_rows(nc.sync, 3)
+
+        for c in range(EARLY):
+            load_chunk(c)
+        word_tables = []
+        for g in range(PASSES):
+            table = sbuf([P, T], U32, f"word_table{g}")
+            nc.sync.dma_start(table[:].bitcast(I32), x_words[g].rearrange("p n t -> p (n t)").bitcast(I32))
+            word_tables.append(table)
+        for c in range(EARLY, CHUNKS):
+            load_chunk(c)
+
+        alpha_rows = sbuf([P, P], F32, "alpha_rows")
+        nc.vector.memset(alpha_rows[:], 0.0)
+        nc.scalar.dma_start(alpha_rows[0:TILES, :], alpha.rearrange("(i p) o -> i (p o)", p=P))
+        warm = sbuf([P, 8], F32, "warm")
+        nc.vector.memset(warm[:], 1.0)
+        warm_out = sbuf([P, 8], F32, "warm_out")
+        nc.scalar.activation(out=warm_out[:], in_=warm[:], func=ACT.Sqrt)
+        identity = sbuf([P, P], F32, "identity")
+        nc.vector.memset(identity[:], 0.0)
+        make_identity(nc, identity[:], nomemset=True)
+        alpha_turned = psum.tile([P, P], F32, name="alpha_turned", tag="z_last1")
+        nc.tensor.transpose(alpha_turned[:], alpha_rows[:], identity[:])
+        alpha_sb = sbuf([P, TILES], F32, "alpha_sb")
+        nc.scalar.copy(out=alpha_sb[:], in_=alpha_turned[:, 0:TILES])
+
+        def interleave(copy, grouped, raw):
+            copy(
+                out=grouped.rearrange("p (c i) t -> p c t i", i=4),
+                in_=raw.rearrange("p t (c i) -> p c t i", i=4),
+            )
+
+        def quantise(grouped, name):
+            width = grouped.shape[1]
+            codes = sbuf([P, width], U32, f"codes_{name}")
+            scales = sbuf([P, width], U8, f"scales_{name}")
+            nc.vector.quantize_mx(out=codes[:].bitcast(FP8X4), scales=scales[:], in_=grouped[:].rearrange("p c t -> p (c t)"))
+            return codes, scales
+
+        front = []
+        for g in range(PASSES):
+            grouped = sbuf([P, V + CW, PACK], BF16, f"front{g}")
+            interleave(nc.vector.tensor_copy, grouped[:, 0:V, :], th_raw[:, g, :].rearrange("p (t v) -> p t v", t=PACK))
+            interleave(nc.scalar.copy, grouped[:, V : V + CW, :], lc_raw[0, g][:])
+            front.append(grouped)
+        x_scale = sbuf([P, S], U8, "x_scale")
+        nc.vector.tensor_copy(x_scale[:], scale_table[:].indirect(offsets[:]))
+        front_mx = [quantise(front[g], f"front{g}") for g in range(PASSES)]
+
+        vector_slot = {1: "word_table1"}
+        scalar_slot = {}
+
+        def prepare(c):
+            grouped = [
+                sbuf([P, CW, PACK], BF16, f"grouped{c}_0", scalar_slot.get(c)),
+                sbuf([P, CW, PACK], BF16, f"grouped{c}_1", vector_slot.get(c)),
+            ]
+            interleave(nc.scalar.copy, grouped[0][:], lc_raw[c, 0][:])
+            interleave(nc.scalar.copy if c < EARLY else nc.vector.tensor_copy, grouped[1][:], lc_raw[c, 1][:])
+            return [quantise(grouped[g], f"lc{c}_{g}") for g in range(PASSES)]
+
+        weights = {c: prepare(c) for c in range(1, EARLY)}
+
+        HALF = S // 2
+        x_codes = [sbuf([P, S], U32, "x_codes0"), sbuf([P, S], U32, "x_codes1", "scale_table")]
+        nc.vector.tensor_copy(x_codes[0][:], word_tables[0][:].indirect(offsets[:]))
+
+        def product(acc, i, g, moving):
+            cols = slice(i * P, (i + 1) * P)
+            nc.tensor.matmul_mx(
+                out=acc,
+                lhsT=x_codes[g][:, cols].bitcast(FP8X4),
+                lhsT_scale=x_scale[4 * g : P, cols],
+                rhs=moving[0][:].bitcast(FP8X4),
+                rhs_scale=moving[1][:],
+                start=(g == 0),
+                stop=(g == PASSES - 1),
+            )
+
+        fronts = [psum.tile([P, V + CW], F32, name=f"front_bank{i}") for i in range(TILES)]
+        for i in range(TILES):
+            product(fronts[i][:], i, 0, front_mx[0])
+        for h in range(2):
+            nc.vector.tensor_copy(x_codes[1][:, h * HALF : (h + 1) * HALF], word_tables[1][:].indirect(offsets[:, h * HALF // 16 : (h + 1) * HALF // 16]))
+            for i in (2 * h, 2 * h + 1):
+                product(fronts[i][:], i, 1, front_mx[1])
+
+        bonus = sbuf([P, TILES, V], F32, "bonus")
+
+        def multiply(c, moving):
+            z = psum.tile([P, TILES, CW], F32, name=f"z{c}")
+            for i in range(TILES):
+                for g in range(PASSES):
+                    product(z[:, i, :], i, g, moving[g])
+            squares = sbuf([P, D, TILES * ARMS], F32, f"squares{c}")
+            nc.scalar.activation(out=squares[:], in_=z[:].rearrange("p i (a d) -> p d (i a)", d=D), func=ACT.Square)
+            return squares
+
+        def lengths(c, squares):
+            pairs = sbuf([P, 2, TILES * ARMS], F32, f"pairs{c}")
+            nc.vector.tensor_add(out=pairs[:], in0=squares[:, 0:2, :], in1=squares[:, 2:4, :])
+            sums = sbuf([P, TILES * ARMS], F32, f"sums{c}")
+            nc.vector.tensor_add(out=sums[:], in0=pairs[:, 0, :], in1=pairs[:, 1, :])
+            nc.scalar.activation(
+                out=bonus[:, :, c * ARMS : (c + 1) * ARMS],
+                in_=sums[:].rearrange("p (i a) -> p i a", i=TILES),
+                func=ACT.Sqrt,
+                bias=0.05,
+            )
+
+        def ready(c):
+            return weights[c] if c in weights else prepare(c)
+
+        squares0 = sbuf([P, D, TILES * ARMS], F32, "squares0")
+        best = sbuf([P, TILES], F32, "best")
+        weights1 = ready(1)
+        for i in range(TILES):
+            nc.scalar.activation(
+                out=squares0[:, :, i * ARMS : (i + 1) * ARMS],
+                in_=fronts[i][:, V : V + CW].rearrange("p (a d) -> p d a", d=D),
+                func=ACT.Square,
+            )
+        squares1 = multiply(1, weights1)
+        weights2 = ready(2)
+        squares2 = multiply(2, weights2)
+        lengths(0, squares0)
+        last = prepare(LAST)
+        banks = [psum.tile([P, 2, CW], F32, name=f"z_last{h}") for h in range(2)]
+        for i in range(TILES):
+            for g in range(PASSES):
+                product(banks[i // 2][:, i % 2, :], i, g, last[g])
+        for i in range(TILES):
+            nc.vector.tensor_reduce(out=best[:, i : i + 1], in_=fronts[i][:, 0:V], axis=AX.X, op=ALU.max)
+        minus_best = sbuf([P, TILES], F32, "minus_best")
+        nc.scalar.mul(out=minus_best[:], in_=best[:], mul=-1.0)
+        lengths(1, squares1)
+        lengths(2, squares2)
+
+        for h in range(2):
+            squares = sbuf([P, 2 * CW], F32, f"squares_last{h}")
+            nc.scalar.activation(out=squares[:], in_=banks[h][:].rearrange("p i c -> p (i c)"), func=ACT.Square)
+            sums = sbuf([P, 2 * ARMS], F32, f"sums_last{h}")
+            nc.vector.tensor_reduce(out=sums[:], in_=squares[:].rearrange("p (a d) -> p a d", d=D), axis=AX.X, op=ALU.add)
+            nc.scalar.activation(
+                out=bonus[:, 2 * h : 2 * h + 2, LAST * ARMS : V], in_=sums[:].rearrange("p (i a) -> p i a", i=2), func=ACT.Sqrt, bias=0.05
+            )
+            for i in (2 * h, 2 * h + 1):
+                ucb = sbuf([P, V], F32, f"ucb{i}")
+                nc.vector.scalar_tensor_tensor(
+                    out=ucb[:], in0=bonus[:, i, :], scalar=alpha_sb[:, i : i + 1], in1=fronts[i][:, 0:V], op0=ALU.mult, op1=ALU.add
+                )
+                gain = sbuf([P, V], F32, f"gain{i}")
+                nc.scalar.activation(out=gain[:], in_=ucb[:], func=ACT.Relu, bias=minus_best[:, i : i + 1])
+                nc.sync.dma_start(out[i * P : (i + 1) * P, :], gain[:])

@@ -22,20 +22,21 @@ PACK = 4
 K_PASS = P * PACK
 PASSES = K // K_PASS
 TILES = S // P
+FRONT = 256
 CW = 128
-CHUNKS = W // CW
-ARMS = CW // D
-LAST = CHUNKS - 1
-EARLY = 1
+HALF = S // 2
 
 
 def tile_picked_ylucb_gain_p_kernel(tc, x_words, x_scales, lc, th, alpha, offs, out):
     nc = tc.nc
     with ExitStack() as ctx:
         keep = ctx.enter_context(tc.tile_pool(name="keep", bufs=1))
+        reuse = ctx.enter_context(tc.tile_pool(name="reuse", bufs=1))
         psum = ctx.enter_context(tc.psum_pool(name="psum", bufs=1))
 
-        def sbuf(shape, dtype, name, slot=None):
+        def sbuf(shape, dtype, name, slot=None, offset=None):
+            if offset is not None:
+                return reuse.tile(shape, dtype, name=name, align_bytes=64, offset=offset)
             return keep.tile(shape, dtype, name=name, tag=slot or name, align_bytes=64)
 
         scale_table = sbuf([P, T], U8, "scale_table")
@@ -47,34 +48,28 @@ def tile_picked_ylucb_gain_p_kernel(tc, x_words, x_scales, lc, th, alpha, offs, 
                 x_scales[:, 4 * q : 4 * q + 4, :].bitcast(I32),
             )
 
+        def load_weights(source, g, first, width, name):
+            raw = sbuf([P, PACK, width], F32, name)
+            rows = source[g * K_PASS : (g + 1) * K_PASS, first : first + width]
+            nc.sync.dma_start(raw[:], rows.rearrange("(p j) c -> p j c", j=PACK))
+            return raw
 
-        lc_raw = {}
-
-        def load_chunk(c):
-            for g in range(PASSES):
-                raw = sbuf([P, PACK, CW], F32, f"lc_raw{c}_{g}")
-                rows = lc[g * K_PASS : (g + 1) * K_PASS, c * CW : (c + 1) * CW]
-                nc.sync.dma_start(raw[:], rows.rearrange("(p j) c -> p j c", j=PACK))
-                lc_raw[c, g] = raw
 
         offsets = keep.tile([P, S // 16], U16, name="offsets")
         nc.sync.dma_start(offsets[:], offs)
-        th_raw = sbuf([P, PASSES, PACK * V], F32, "th_raw")
-        nc.sync.dma_start(th_raw[:], th.rearrange("(g p j) v -> p g (j v)", g=PASSES, j=PACK))
+        front_raw = [load_weights(lc, 0, 0, FRONT, "front_raw0")]
         load_scale_rows(nc.sync, 0)
         load_scale_rows(nc.sync, 1)
         load_scale_rows(nc.sync, 2)
         load_scale_rows(nc.sync, 3)
 
-        for c in range(EARLY):
-            load_chunk(c)
-        word_tables = []
+        front_raw.append(load_weights(lc, 1, 0, FRONT, "front_raw1"))
+        word_tables = [sbuf([P, T], U32, "word_table0"), sbuf([P, T], U32, "word_table1", offset=0)]
         for g in range(PASSES):
-            table = sbuf([P, T], U32, f"word_table{g}")
-            nc.sync.dma_start(table[:].bitcast(I32), x_words[g].rearrange("p n t -> p (n t)").bitcast(I32))
-            word_tables.append(table)
-        for c in range(EARLY, CHUNKS):
-            load_chunk(c)
+            nc.sync.dma_start(word_tables[g][:].bitcast(I32), x_words[g].rearrange("p n t -> p (n t)").bitcast(I32))
+        mid_raw = [load_weights(lc, g, FRONT, CW, f"mid_raw{g}") for g in range(PASSES)]
+        last_raw = [load_weights(lc, g, FRONT + CW, CW, f"last_raw{g}") for g in range(PASSES)]
+        th_raw = [load_weights(th, g, 0, V, f"th_raw{g}") for g in range(PASSES)]
 
         alpha_rows = sbuf([P, P], F32, "alpha_rows")
         nc.vector.memset(alpha_rows[:], 0.0)
@@ -86,49 +81,32 @@ def tile_picked_ylucb_gain_p_kernel(tc, x_words, x_scales, lc, th, alpha, offs, 
         identity = sbuf([P, P], F32, "identity")
         nc.vector.memset(identity[:], 0.0)
         make_identity(nc, identity[:], nomemset=True)
-        alpha_turned = psum.tile([P, P], F32, name="alpha_turned", tag="z_last1")
+        alpha_turned = psum.tile([P, P], F32, name="alpha_turned")
         nc.tensor.transpose(alpha_turned[:], alpha_rows[:], identity[:])
         alpha_sb = sbuf([P, TILES], F32, "alpha_sb")
         nc.scalar.copy(out=alpha_sb[:], in_=alpha_turned[:, 0:TILES])
 
-        def interleave(copy, grouped, raw):
+        def interleave(copy, raw, name, slot=None, offset=None):
+            grouped = sbuf([P, raw.shape[2], PACK], BF16, name, slot, offset)
             copy(
-                out=grouped.rearrange("p (c i) t -> p c t i", i=4),
-                in_=raw.rearrange("p t (c i) -> p c t i", i=4),
+                out=grouped[:].rearrange("p (c i) t -> p c t i", i=4),
+                in_=raw[:].rearrange("p t (c i) -> p c t i", i=4),
             )
+            return grouped
 
-        def quantise(grouped, name):
+        def quantise(grouped, name, offset=None):
             width = grouped.shape[1]
-            codes = sbuf([P, width], U32, f"codes_{name}")
+            codes = sbuf([P, width], U32, f"codes_{name}", offset=offset)
             scales = sbuf([P, width], U8, f"scales_{name}")
             nc.vector.quantize_mx(out=codes[:].bitcast(FP8X4), scales=scales[:], in_=grouped[:].rearrange("p c t -> p (c t)"))
             return codes, scales
 
-        front = []
-        for g in range(PASSES):
-            grouped = sbuf([P, V + CW, PACK], BF16, f"front{g}")
-            interleave(nc.vector.tensor_copy, grouped[:, 0:V, :], th_raw[:, g, :].rearrange("p (t v) -> p t v", t=PACK))
-            interleave(nc.scalar.copy, grouped[:, V : V + CW, :], lc_raw[0, g][:])
-            front.append(grouped)
+        front_grouped = [interleave(nc.vector.tensor_copy, front_raw[0], "front0"), interleave(nc.scalar.copy, front_raw[1], "front1")]
+        front_mx = [quantise(front_grouped[0], "front0")]
         x_scale = sbuf([P, S], U8, "x_scale")
         nc.vector.tensor_copy(x_scale[:], scale_table[:].indirect(offsets[:]))
-        front_mx = [quantise(front[g], f"front{g}") for g in range(PASSES)]
+        front_mx.append(quantise(front_grouped[1], "front1"))
 
-        vector_slot = {1: "word_table1"}
-        scalar_slot = {}
-
-        def prepare(c):
-            grouped = [
-                sbuf([P, CW, PACK], BF16, f"grouped{c}_0", scalar_slot.get(c)),
-                sbuf([P, CW, PACK], BF16, f"grouped{c}_1", vector_slot.get(c)),
-            ]
-            interleave(nc.scalar.copy, grouped[0][:], lc_raw[c, 0][:])
-            interleave(nc.scalar.copy if c < EARLY else nc.vector.tensor_copy, grouped[1][:], lc_raw[c, 1][:])
-            return [quantise(grouped[g], f"lc{c}_{g}") for g in range(PASSES)]
-
-        weights = {c: prepare(c) for c in range(1, EARLY)}
-
-        HALF = S // 2
         x_codes = [sbuf([P, S], U32, "x_codes0"), sbuf([P, S], U32, "x_codes1", "scale_table")]
         nc.vector.tensor_copy(x_codes[0][:], word_tables[0][:].indirect(offsets[:]))
 
@@ -144,7 +122,7 @@ def tile_picked_ylucb_gain_p_kernel(tc, x_words, x_scales, lc, th, alpha, offs, 
                 stop=(g == PASSES - 1),
             )
 
-        fronts = [psum.tile([P, V + CW], F32, name=f"front_bank{i}") for i in range(TILES)]
+        fronts = [psum.tile([P, FRONT], F32, name=f"front_bank{i}", tag=f"bank{i}") for i in range(TILES)]
         for i in range(TILES):
             product(fronts[i][:], i, 0, front_mx[0])
         for h in range(2):
@@ -154,68 +132,76 @@ def tile_picked_ylucb_gain_p_kernel(tc, x_words, x_scales, lc, th, alpha, offs, 
 
         bonus = sbuf([P, TILES, V], F32, "bonus")
 
-        def multiply(c, moving):
-            z = psum.tile([P, TILES, CW], F32, name=f"z{c}")
-            for i in range(TILES):
-                for g in range(PASSES):
-                    product(z[:, i, :], i, g, moving[g])
-            squares = sbuf([P, D, TILES * ARMS], F32, f"squares{c}")
-            nc.scalar.activation(out=squares[:], in_=z[:].rearrange("p i (a d) -> p d (i a)", d=D), func=ACT.Square)
-            return squares
-
-        def lengths(c, squares):
-            pairs = sbuf([P, 2, TILES * ARMS], F32, f"pairs{c}")
+        def lengths(squares, first, name):
+            arms = squares.shape[2] // TILES
+            pairs = sbuf([P, 2, TILES * arms], F32, f"pairs_{name}")
             nc.vector.tensor_add(out=pairs[:], in0=squares[:, 0:2, :], in1=squares[:, 2:4, :])
-            sums = sbuf([P, TILES * ARMS], F32, f"sums{c}")
+            sums = sbuf([P, TILES * arms], F32, f"sums_{name}")
             nc.vector.tensor_add(out=sums[:], in0=pairs[:, 0, :], in1=pairs[:, 1, :])
             nc.scalar.activation(
-                out=bonus[:, :, c * ARMS : (c + 1) * ARMS],
+                out=bonus[:, :, first : first + arms],
                 in_=sums[:].rearrange("p (i a) -> p i a", i=TILES),
                 func=ACT.Sqrt,
                 bias=0.05,
             )
 
-        def ready(c):
-            return weights[c] if c in weights else prepare(c)
+        mid_grouped = [interleave(nc.scalar.copy, mid_raw[0], "mid0"), interleave(nc.vector.tensor_copy, mid_raw[1], "mid1", offset=0)]
+        mid_mx = [quantise(mid_grouped[0], "mid0", offset=2048), quantise(mid_grouped[1], "mid1")]
 
-        squares0 = sbuf([P, D, TILES * ARMS], F32, "squares0")
-        best = sbuf([P, TILES], F32, "best")
-        weights1 = ready(1)
+        front_arms = FRONT // D
+        front_squares = sbuf([P, D, TILES * front_arms], F32, "front_squares")
         for i in range(TILES):
             nc.scalar.activation(
-                out=squares0[:, :, i * ARMS : (i + 1) * ARMS],
-                in_=fronts[i][:, V : V + CW].rearrange("p (a d) -> p d a", d=D),
+                out=front_squares[:, :, i * front_arms : (i + 1) * front_arms],
+                in_=fronts[i][:].rearrange("p (a d) -> p d a", d=D),
                 func=ACT.Square,
             )
-        squares1 = multiply(1, weights1)
-        weights2 = ready(2)
-        squares2 = multiply(2, weights2)
-        lengths(0, squares0)
-        last = prepare(LAST)
-        banks = [psum.tile([P, 2, CW], F32, name=f"z_last{h}") for h in range(2)]
+
+        arms = CW // D
+        mid = psum.tile([P, TILES, CW], F32, name="mid")
         for i in range(TILES):
             for g in range(PASSES):
-                product(banks[i // 2][:, i % 2, :], i, g, last[g])
-        for i in range(TILES):
-            nc.vector.tensor_reduce(out=best[:, i : i + 1], in_=fronts[i][:, 0:V], axis=AX.X, op=ALU.max)
-        minus_best = sbuf([P, TILES], F32, "minus_best")
-        nc.scalar.mul(out=minus_best[:], in_=best[:], mul=-1.0)
-        lengths(1, squares1)
-        lengths(2, squares2)
+                product(mid[:, i, :], i, g, mid_mx[g])
+        mid_squares = sbuf([P, D, TILES * arms], F32, "mid_squares")
+        nc.scalar.activation(out=mid_squares[:], in_=mid[:].rearrange("p i (a d) -> p d (i a)", d=D), func=ACT.Square)
 
+        last_grouped = [interleave(nc.scalar.copy, last_raw[0], "last0", "mid0"), interleave(nc.vector.tensor_copy, last_raw[1], "last1", offset=1024)]
+        last_mx = [quantise(last_grouped[g], f"last{g}") for g in range(PASSES)]
+        lasts = [psum.tile([P, 2, CW], F32, name=f"last_bank{h}") for h in range(2)]
+        for i in range(TILES):
+            for g in range(PASSES):
+                product(lasts[i // 2][:, i % 2, :], i, g, last_mx[g])
+
+        lengths(front_squares, 0, "front")
+
+        th_grouped = [interleave(nc.scalar.copy, th_raw[0], "th0", offset=0), interleave(nc.vector.tensor_copy, th_raw[1], "th1", "front_squares")]
+        th_mx = [quantise(th_grouped[g], f"th{g}") for g in range(PASSES)]
+        means = [psum.tile([P, V], F32, name=f"mean_bank{i}", tag=f"bank{i}") for i in range(TILES)]
+        for g in range(PASSES):
+            for i in range(TILES):
+                product(means[i][:], i, g, th_mx[g])
+
+        lengths(mid_squares, front_arms, "mid")
         for h in range(2):
-            squares = sbuf([P, 2 * CW], F32, f"squares_last{h}")
-            nc.scalar.activation(out=squares[:], in_=banks[h][:].rearrange("p i c -> p (i c)"), func=ACT.Square)
-            sums = sbuf([P, 2 * ARMS], F32, f"sums_last{h}")
+            squares = sbuf([P, 2 * CW], F32, f"last_squares{h}")
+            nc.scalar.activation(out=squares[:], in_=lasts[h][:].rearrange("p i c -> p (i c)"), func=ACT.Square)
+            sums = sbuf([P, 2 * arms], F32, f"last_sums{h}")
             nc.vector.tensor_reduce(out=sums[:], in_=squares[:].rearrange("p (a d) -> p a d", d=D), axis=AX.X, op=ALU.add)
             nc.scalar.activation(
-                out=bonus[:, 2 * h : 2 * h + 2, LAST * ARMS : V], in_=sums[:].rearrange("p (i a) -> p i a", i=2), func=ACT.Sqrt, bias=0.05
+                out=bonus[:, 2 * h : 2 * h + 2, V - arms : V], in_=sums[:].rearrange("p (i a) -> p i a", i=2), func=ACT.Sqrt, bias=0.05
             )
-            for i in (2 * h, 2 * h + 1):
-                ucb = sbuf([P, V], F32, f"ucb{i}")
-                nc.vector.scalar_tensor_tensor(
-                    out=ucb[:], in0=bonus[:, i, :], scalar=alpha_sb[:, i : i + 1], in1=fronts[i][:, 0:V], op0=ALU.mult, op1=ALU.add
-                )
-                gain = sbuf([P, V], F32, f"gain{i}")
-                nc.scalar.activation(out=gain[:], in_=ucb[:], func=ACT.Relu, bias=minus_best[:, i : i + 1])
-                nc.sync.dma_start(out[i * P : (i + 1) * P, :], gain[:])
+
+        minus_best = []
+        for i in range(TILES):
+            best = sbuf([P, 1], F32, f"best{i}")
+            nc.vector.tensor_reduce(out=best[:], in_=means[i][:], axis=AX.X, op=ALU.max)
+            minus_best.append(sbuf([P, 1], F32, f"minus_best{i}"))
+            nc.scalar.mul(out=minus_best[i][:], in_=best[:], mul=-1.0)
+        for i in range(TILES):
+            ucb = sbuf([P, V], F32, f"ucb{i}")
+            nc.vector.scalar_tensor_tensor(
+                out=ucb[:], in0=bonus[:, i, :], scalar=alpha_sb[:, i : i + 1], in1=means[i][:], op0=ALU.mult, op1=ALU.add
+            )
+            gain = sbuf([P, V], F32, f"gain{i}")
+            nc.scalar.activation(out=gain[:], in_=ucb[:], func=ACT.Relu, bias=minus_best[i][:])
+            nc.sync.dma_start(out[i * P : (i + 1) * P, :], gain[:])

from contextlib import ExitStack

import concourse.mybir as mybir
from concourse.masks import make_identity

K, T, S, V, D, W = 1024, 2048, 512, 128, 4, 512
FLOPS = 2 * K * S * (V + W)

F32 = mybir.dt.float32
BF16 = mybir.dt.bfloat16
I32 = mybir.dt.int32
U32 = mybir.dt.uint32
U16 = mybir.dt.uint16
U8 = mybir.dt.uint8
FP8X4 = mybir.dt.float8_e4m3fn_x4
ACT = mybir.ActivationFunctionType
ALU = mybir.AluOpType
AX = mybir.AxisListType

P = 128
PACK = 4
K_PASS = P * PACK
PASSES = K // K_PASS
TILES = S // P
FRONT = 256
CW = 128
HALF = S // 2


def tile_picked_ylucb_gain_p_kernel(tc, x_words, x_scales, lc, th, alpha, offs, out):
    nc = tc.nc
    with ExitStack() as ctx:
        keep = ctx.enter_context(tc.tile_pool(name="keep", bufs=1))
        reuse = ctx.enter_context(tc.tile_pool(name="reuse", bufs=1))
        psum = ctx.enter_context(tc.psum_pool(name="psum", bufs=1))

        def sbuf(shape, dtype, name, slot=None, offset=None):
            if offset is not None:
                return reuse.tile(shape, dtype, name=name, align_bytes=64, offset=offset)
            return keep.tile(shape, dtype, name=name, tag=slot or name, align_bytes=64)

        scale_table = sbuf([P, T], U8, "scale_table")
        nc.gpsimd.memset(scale_table[:].bitcast(I32), 0)

        def load_scale_rows(queue, q):
            queue.dma_start(
                scale_table[32 * q : 32 * q + 4 * PASSES, :].bitcast(I32),
                x_scales[:, 4 * q : 4 * q + 4, :].bitcast(I32),
            )

        def load_weights(source, g, first, width, name):
            raw = sbuf([P, PACK, width], F32, name)
            rows = source[g * K_PASS : (g + 1) * K_PASS, first : first + width]
            nc.sync.dma_start(raw[:], rows.rearrange("(p j) c -> p j c", j=PACK))
            return raw


        offsets = keep.tile([P, S // 16], U16, name="offsets")
        nc.sync.dma_start(offsets[:], offs)
        front_raw = [load_weights(lc, 0, 0, FRONT, "front_raw0")]
        load_scale_rows(nc.sync, 0)
        load_scale_rows(nc.sync, 1)
        load_scale_rows(nc.sync, 2)
        load_scale_rows(nc.sync, 3)

        front_raw.append(load_weights(lc, 1, 0, FRONT, "front_raw1"))
        word_tables = [sbuf([P, T], U32, "word_table0"), sbuf([P, T], U32, "word_table1", offset=0)]
        for g in range(PASSES):
            nc.sync.dma_start(word_tables[g][:].bitcast(I32), x_words[g].rearrange("p n t -> p (n t)").bitcast(I32))
        mid_raw = [load_weights(lc, g, FRONT, CW, f"mid_raw{g}") for g in range(PASSES)]
        last_raw = [load_weights(lc, g, FRONT + CW, CW, f"last_raw{g}") for g in range(PASSES)]
        th_raw = [load_weights(th, g, 0, V, f"th_raw{g}") for g in range(PASSES)]

        alpha_rows = sbuf([P, P], F32, "alpha_rows")
        nc.vector.memset(alpha_rows[:], 0.0)
        nc.scalar.dma_start(alpha_rows[0:TILES, :], alpha.rearrange("(i p) o -> i (p o)", p=P))
        warm = sbuf([P, 8], F32, "warm")
        nc.vector.memset(warm[:], 1.0)
        warm_out = sbuf([P, 8], F32, "warm_out")
        nc.scalar.activation(out=warm_out[:], in_=warm[:], func=ACT.Sqrt)
        identity = sbuf([P, P], F32, "identity")
        nc.vector.memset(identity[:], 0.0)
        make_identity(nc, identity[:], nomemset=True)
        alpha_turned = psum.tile([P, P], F32, name="alpha_turned")
        nc.tensor.transpose(alpha_turned[:], alpha_rows[:], identity[:])
        alpha_sb = sbuf([P, TILES], F32, "alpha_sb")
        nc.scalar.copy(out=alpha_sb[:], in_=alpha_turned[:, 0:TILES])

        def interleave(copy, raw, name, slot=None, offset=None):
            grouped = sbuf([P, raw.shape[2], PACK], BF16, name, slot, offset)
            copy(
                out=grouped[:].rearrange("p (c i) t -> p c t i", i=4),
                in_=raw[:].rearrange("p t (c i) -> p c t i", i=4),
            )
            return grouped

        def quantise(grouped, name, offset=None):
            width = grouped.shape[1]
            codes = sbuf([P, width], U32, f"codes_{name}", offset=offset)
            scales = sbuf([P, width], U8, f"scales_{name}")
            nc.vector.quantize_mx(out=codes[:].bitcast(FP8X4), scales=scales[:], in_=grouped[:].rearrange("p c t -> p (c t)"))
            return codes, scales

        front_grouped = [interleave(nc.vector.tensor_copy, front_raw[0], "front0"), interleave(nc.scalar.copy, front_raw[1], "front1")]
        front_mx = [quantise(front_grouped[0], "front0")]
        x_scale = sbuf([P, S], U8, "x_scale")
        nc.vector.tensor_copy(x_scale[:], scale_table[:].indirect(offsets[:]))
        front_mx.append(quantise(front_grouped[1], "front1"))

        x_codes = [sbuf([P, S], U32, "x_codes0"), sbuf([P, S], U32, "x_codes1", "scale_table")]
        nc.vector.tensor_copy(x_codes[0][:], word_tables[0][:].indirect(offsets[:]))

        def product(acc, i, g, moving):
            cols = slice(i * P, (i + 1) * P)
            nc.tensor.matmul_mx(
                out=acc,
                lhsT=x_codes[g][:, cols].bitcast(FP8X4),
                lhsT_scale=x_scale[4 * g : P, cols],
                rhs=moving[0][:].bitcast(FP8X4),
                rhs_scale=moving[1][:],
                start=(g == 0),
                stop=(g == PASSES - 1),
            )

        fronts = [psum.tile([P, FRONT], F32, name=f"front_bank{i}", tag=f"bank{i}") for i in range(TILES)]
        for i in range(TILES):
            product(fronts[i][:], i, 0, front_mx[0])
        for h in range(2):
            nc.vector.tensor_copy(x_codes[1][:, h * HALF : (h + 1) * HALF], word_tables[1][:].indirect(offsets[:, h * HALF // 16 : (h + 1) * HALF // 16]))
            for i in (2 * h, 2 * h + 1):
                product(fronts[i][:], i, 1, front_mx[1])

        bonus = sbuf([P, TILES, V], F32, "bonus")

        def lengths(squares, first, name):
            arms = squares.shape[2] // TILES
            pairs = sbuf([P, 2, TILES * arms], F32, f"pairs_{name}")
            nc.vector.tensor_add(out=pairs[:], in0=squares[:, 0:2, :], in1=squares[:, 2:4, :])
            sums = sbuf([P, TILES * arms], F32, f"sums_{name}")
            nc.vector.tensor_add(out=sums[:], in0=pairs[:, 0, :], in1=pairs[:, 1, :])
            nc.scalar.activation(
                out=bonus[:, :, first : first + arms],
                in_=sums[:].rearrange("p (i a) -> p i a", i=TILES),
                func=ACT.Sqrt,
                bias=0.05,
            )

        mid_grouped = [interleave(nc.scalar.copy, mid_raw[0], "mid0"), interleave(nc.vector.tensor_copy, mid_raw[1], "mid1", offset=0)]
        mid_mx = [quantise(mid_grouped[0], "mid0", offset=2048), quantise(mid_grouped[1], "mid1")]

        front_arms = FRONT // D
        front_squares = sbuf([P, D, TILES * front_arms], F32, "front_squares")
        for i in range(TILES):
            nc.scalar.activation(
                out=front_squares[:, :, i * front_arms : (i + 1) * front_arms],
                in_=fronts[i][:].rearrange("p (a d) -> p d a", d=D),
                func=ACT.Square,
            )

        arms = CW // D
        mid = psum.tile([P, TILES, CW], F32, name="mid")
        for i in range(TILES):
            for g in range(PASSES):
                product(mid[:, i, :], i, g, mid_mx[g])
        mid_squares = sbuf([P, D, TILES * arms], F32, "mid_squares")
        nc.scalar.activation(out=mid_squares[:], in_=mid[:].rearrange("p i (a d) -> p d (i a)", d=D), func=ACT.Square)

        last_grouped = [interleave(nc.scalar.copy, last_raw[0], "last0", "mid0"), interleave(nc.vector.tensor_copy, last_raw[1], "last1", offset=1024)]
        last_mx = [quantise(last_grouped[g], f"last{g}") for g in range(PASSES)]
        lasts = [psum.tile([P, 2, CW], F32, name=f"last_bank{h}") for h in range(2)]
        for i in range(TILES):
            for g in range(PASSES):
                product(lasts[i // 2][:, i % 2, :], i, g, last_mx[g])

        lengths(front_squares, 0, "front")

        th_grouped = [interleave(nc.scalar.copy, th_raw[0], "th0", offset=0), interleave(nc.vector.tensor_copy, th_raw[1], "th1", "front_squares")]
        th_mx = [quantise(th_grouped[g], f"th{g}") for g in range(PASSES)]
        means = [psum.tile([P, V], F32, name=f"mean_bank{i}", tag=f"bank{i}") for i in range(TILES)]
        for g in range(PASSES):
            for i in range(TILES):
                product(means[i][:], i, g, th_mx[g])

        lengths(mid_squares, front_arms, "mid")
        for h in range(2):
            squares = sbuf([P, 2 * CW], F32, f"last_squares{h}")
            nc.scalar.activation(out=squares[:], in_=lasts[h][:].rearrange("p i c -> p (i c)"), func=ACT.Square)
            sums = sbuf([P, 2 * arms], F32, f"last_sums{h}")
            nc.vector.tensor_reduce(out=sums[:], in_=squares[:].rearrange("p (a d) -> p a d", d=D), axis=AX.X, op=ALU.add)
            nc.scalar.activation(
                out=bonus[:, 2 * h : 2 * h + 2, V - arms : V], in_=sums[:].rearrange("p (i a) -> p i a", i=2), func=ACT.Sqrt, bias=0.05
            )

        minus_best = []
        for i in range(TILES):
            best = sbuf([P, 1], F32, f"best{i}")
            nc.vector.tensor_reduce(out=best[:], in_=means[i][:], axis=AX.X, op=ALU.max)
            minus_best.append(sbuf([P, 1], F32, f"minus_best{i}"))
            nc.scalar.mul(out=minus_best[i][:], in_=best[:], mul=-1.0)
        for i in range(TILES):
            ucb = sbuf([P, V], F32, f"ucb{i}")
            nc.vector.scalar_tensor_tensor(
                out=ucb[:], in0=bonus[:, i, :], scalar=alpha_sb[:, i : i + 1], in1=means[i][:], op0=ALU.mult, op1=ALU.add
            )
            gain = sbuf([P, V], F32, f"gain{i}")
            nc.scalar.activation(out=gain[:], in_=ucb[:], func=ACT.Relu, bias=minus_best[i][:])
            nc.sync.dma_start(out[i * P : (i + 1) * P, :], gain[:])
